import numpy as np
import ml_dtypes


def mxq(x, axis, fmt="e4m3"):
    dtype, down = {"e4m3": (ml_dtypes.float8_e4m3fn, 7), "e5m2": (ml_dtypes.float8_e5m2, 14)}[fmt]
    v = np.moveaxis(np.asarray(x, np.float32).astype(ml_dtypes.bfloat16).astype(np.float64), axis, -1)
    blocks = v.reshape(v.shape[:-1] + (-1, 32))
    amax = np.abs(blocks).max(-1, keepdims=True)
    byte = np.maximum(np.where(amax > 0, np.frexp(amax)[1] - 1 + 127, 0) - down, 1)
    scale = np.exp2(byte - 127.0)
    codes = (blocks / scale).astype(np.float32).astype(dtype).astype(np.float64)
    return np.moveaxis((codes * scale).reshape(v.shape), -1, axis)


WIDE = False


def mx_kscale(k):
    if not WIDE:
        return np.ones(k)
    levels = np.array([10, -10, 5, -5, 0])
    if k % 512:
        return np.exp2(np.random.permutation(np.resize(levels, k // 32))).repeat(32)
    a = np.empty((k // 512, 16))
    for p in range(k // 512):
        a[p, :8] = np.random.permutation(np.resize(levels, 8))
        for g in range(8):
            far = levels[np.abs(levels - a[p, g]) >= 10]
            a[p, g + 8] = far[np.random.randint(len(far))]
    return np.exp2(a.ravel()).repeat(32)


def f64(x):
    return np.asarray(x).astype(np.float64)


def striped(idx):
    return np.tile(idx.reshape(-1, 16).T, (8, 1)).astype(np.uint16)


def unstriped(offs):
    return offs[:16].T.reshape(-1).astype(np.int64)


def pack_weight(w):
    k, n = w.shape
    w = f64(np.asarray(w, np.float32).astype(ml_dtypes.bfloat16)).reshape(k // 32, 32, n)
    amax = np.abs(w).max(1)
    byte = np.clip(np.where(amax > 0, np.frexp(amax)[1] - 1 + 127 - 7, 1), 1, 254)
    scaled = (w * np.exp2(127.0 - byte)[:, None, :]).reshape(k, n).astype(np.float32)
    words = np.ascontiguousarray(scaled.reshape(k // 512, 128, 4, n).transpose(0, 1, 3, 2)).astype(ml_dtypes.float8_e4m3fn).view(np.uint8)
    return words, np.ascontiguousarray(byte.astype(np.uint8).reshape(k // 512, 16, n))


def unpack_weight(words, scales):
    g, p, n, _ = words.shape
    vals = np.ascontiguousarray(words).view(ml_dtypes.float8_e4m3fn).astype(np.float64) * np.repeat(np.exp2(scales.astype(np.float64) - 127.0), 8, axis=1)[..., None]
    return vals.transpose(0, 1, 3, 2).reshape(g * 512, n)


K, T, E, C, N = 1536, 1536, 6, 128, 128


def by_expert(wq, xq):
    return np.concatenate([wq[e].T @ xq[:, e * C:(e + 1) * C] for e in range(E)], axis=1)


def setup_inputs():
    n = np.random.standard_normal
    s = mx_kscale(K)[:, None]
    packed = [pack_weight(m) for m in n((E, K, N)) / np.sqrt(K) / s[None]]
    return {
        "xT": (n((K, T)) * s).astype(np.float32),
        "w_words": np.stack([m[0] for m in packed]),
        "w_scales": np.stack([m[1] for m in packed]),
        "gate": np.tile(np.random.uniform(0.2, 1.0, E * C), (N, 1)).astype(np.float32),
        "offs": striped(np.random.permutation(T)[:E * C]),
        "dst": striped(np.random.permutation(T)[:E * C]),
    }


def reference(xT, w_words, w_scales, gate, offs, dst):
    idx = unstriped(offs)
    w = np.stack([unpack_weight(w_words[e], w_scales[e]) for e in range(E)])
    xq = mxq(f64(xT)[:, idx], 0, "e4m3")
    y = by_expert(w, xq)
    out = np.zeros((N, T))
    out[:, unstriped(dst)] = f64(gate) * y
    return out

@@ -1,0 +1,137 @@
+import concourse.mybir as mybir
+
+E, C, K, T, N = 6, 128, 1536, 1536, 128
+S = E * C
+P = 128
+PACK = 4
+PASSES = 3
+
+F32 = mybir.dt.float32
+BF16 = mybir.dt.bfloat16
+U32 = mybir.dt.uint32
+I32 = mybir.dt.int32
+U16 = mybir.dt.uint16
+U8 = mybir.dt.uint8
+FP8X4 = mybir.dt.float8_e4m3fn_x4
+COPY = mybir.ActivationFunctionType.Copy
+MULT = mybir.AluOpType.mult
+
+FLOPS = 2 * K * S * N
+
+CHUNKS = (
+    (0, 0, 256, 64), (0, 256, 256, 64), (0, 512, 512, 128), (0, 1024, 512, 128),
+    (1, 0, 512, 128), (1, 512, 512, 128), (1, 1024, 512, 128),
+    (2, 0, 512, 128), (2, 512, 512, 128), (2, 1024, 256, 128), (2, 1280, 256, 160),
+)
+
+
+def tile_moe_two_lin_none_kernel(tc, xT, w_words, w_scales, gate, offs, dst, out):
+    nc = tc.nc
+    half = S // 2
+    with (
+        tc.tile_pool(name="keep", bufs=1) as keep,
+        tc.psum_pool(name="psum", bufs=1) as psum,
+    ):
+        gather_list = keep.tile([P, S // 16], U16, name="gather_list")
+        scatter_list = keep.tile([P, S // 16], U16, name="scatter_list")
+
+        w_plane = keep.tile([P, E * PASSES, N], U8, align_bytes=256, name="w_plane")
+        plane = keep.tile([P, T], U8, align_bytes=256, name="plane")
+        result = keep.tile([P, T], F32, align_bytes=256, name="result")
+        nc.vector.memset(w_plane[:].bitcast(I32), 0)
+        nc.gpsimd.memset(plane[:], 0)
+        nc.gpsimd.memset(result[:], 0.0)
+
+        x_view = xT.rearrange("(a p j) t -> a p j t", a=PASSES, j=PACK)
+        raw = []
+        for i, (a, t0, width, vector_width) in enumerate(CHUNKS):
+            x_chunk = keep.tile([P, PACK, width], F32, align_bytes=256, name=f"x_chunk{i}")
+            nc.sync.dma_start(x_chunk[:], x_view[a, :, :, t0 : t0 + width])
+            raw.append(x_chunk)
+            if i == 2:
+                nc.sync.dma_start(gather_list[:], offs)
+                nc.sync.dma_start(scatter_list[:], dst)
+
+        scale_rows = w_scales.rearrange("e a (s r) n -> s r (e a) n", r=4)
+        for s in range(4):
+            nc.sync.dma_start(w_plane[32 * s : 32 * s + 4].bitcast(I32), scale_rows[s].bitcast(I32))
+        w_codes = []
+        gates = []
+        for e in range(E):
+            w_code = keep.tile([P, PASSES, N], U32, align_bytes=256, name=f"w_code{e}")
+            nc.sync.dma_start(w_code[:].bitcast(I32), w_words[e].rearrange("a p n r -> p a (n r)").bitcast(I32))
+            w_codes.append(w_code)
+            if e % 3 == 2:
+                h = e // 3
+                gate_half = keep.tile([P, half], F32, align_bytes=256, name=f"gate_half{h}")
+                nc.sync.dma_start(gate_half[:], gate[:, h * half : (h + 1) * half])
+                gates.append(gate_half)
+
+        codes = []
+        for a in range(PASSES):
+            pass_codes = keep.tile([P, T], U32, align_bytes=256, name=f"pass_codes{a}")
+            codes.append(pass_codes)
+        slot_codes = []
+        for a in range(PASSES):
+            slot_code = keep.tile([P, S], U32, align_bytes=256, name=f"slot_code{a}")
+            slot_codes.append(slot_code)
+        slot_plane = keep.tile([P, S], U8, align_bytes=256, name="slot_plane")
+
+        def interleaved(ap):
+            return ap.rearrange("p (c i) j -> p c j i", i=4)
+
+        def by_four(ap):
+            return ap.rearrange("p j (c i) -> p c j i", i=4)
+
+        grouped = []
+
+        def round_chunk(i):
+            a, t0, width, v = CHUNKS[i]
+            group = keep.tile([P, width, PACK], BF16, align_bytes=256, name=f"group{i}")
+            nc.scalar.activation(interleaved(group[:, v:width, :]), by_four(raw[i][:, :, v:width]), COPY)
+            nc.vector.tensor_copy(interleaved(group[:, 0:v, :]), by_four(raw[i][:, :, 0:v]))
+            grouped.append(group)
+
+        def quantize_chunk(i):
+            a, t0, width, v = CHUNKS[i]
+            nc.vector.quantize_mx(
+                out=codes[a][:, t0 : t0 + width].bitcast(FP8X4),
+                scales=plane[4 * a : P, t0 : t0 + width],
+                in_=grouped[i][:].rearrange("p w j -> p (w j)"),
+            )
+            if t0 + width == T and a < PASSES - 1:
+                nc.vector.tensor_copy(slot_codes[a][:], codes[a][:].indirect(gather_list[:]))
+
+        round_chunk(0)
+        for i in range(1, len(CHUNKS)):
+            round_chunk(i)
+            quantize_chunk(i - 1)
+        quantize_chunk(len(CHUNKS) - 1)
+
+        last = PASSES - 1
+        for h in range(2):
+            cols = slice(h * half, (h + 1) * half)
+            entries = slice(h * half // 16, (h + 1) * half // 16)
+            nc.vector.tensor_copy(slot_codes[last][:, cols], codes[last][:].indirect(gather_list[:, entries]))
+            nc.vector.tensor_copy(slot_plane[:, cols], plane[:].indirect(gather_list[:, entries]))
+        for h in range(2):
+            acc = psum.tile([P, half], F32, name=f"acc{h}")
+            for local in range(3):
+                e = 3 * h + local
+                slots = slice(e * C, (e + 1) * C)
+                for a in range(PASSES):
+                    nc.tensor.matmul_mx(
+                        out=acc[:, local * C : (local + 1) * C],
+                        lhsT=w_codes[e][:, a, :].bitcast(FP8X4),
+                        lhsT_scale=w_plane[:, PASSES * e + a, :],
+                        rhs=slot_codes[a][:, slots].bitcast(FP8X4),
+                        rhs_scale=slot_plane[4 * a : P, slots],
+                        start=(a == 0),
+                        stop=(a == PASSES - 1),
+                    )
+            y = keep.tile([P, half], F32, align_bytes=256, name=f"y{h}")
+            nc.scalar.activation(y[:], acc[:], COPY)
+            nc.vector.tensor_tensor(
+                result[:].indirect(scatter_list[:, h * half // 16 : (h + 1) * half // 16]), y[:], gates[h][:], MULT
+            )
+        nc.sync.dma_start(out, result[:])

@@ -19,15 +19,16 @@ MULT = mybir.AluOpType.mult
 FLOPS = 2 * K * S * N
 
 CHUNKS = (
-    (0, 0, 256, 64), (0, 256, 256, 64), (0, 512, 512, 128), (0, 1024, 512, 128),
-    (1, 0, 512, 128), (1, 512, 512, 128), (1, 1024, 512, 128),
-    (2, 0, 512, 128), (2, 512, 512, 128), (2, 1024, 256, 128), (2, 1280, 256, 160),
+    (0, 0, 768, 192), (0, 768, 768, 192),
+    (1, 0, 768, 192), (1, 768, 768, 192),
+    (2, 0, 768, 192), (2, 768, 512, 256), (2, 1280, 256, 160),
 )
+PARTS = 3
 
 
 def tile_moe_two_lin_none_kernel(tc, xT, w_words, w_scales, gate, offs, dst, out):
     nc = tc.nc
-    half = S // 2
+    part = S // PARTS
     with (
         tc.tile_pool(name="keep", bufs=1) as keep,
         tc.psum_pool(name="psum", bufs=1) as psum,
@@ -48,7 +49,7 @@ def tile_moe_two_lin_none_kernel(tc, xT, w_words, w_scales, gate, offs, dst, out
             x_chunk = keep.tile([P, PACK, width], F32, align_bytes=256, name=f"x_chunk{i}")
             nc.sync.dma_start(x_chunk[:], x_view[a, :, :, t0 : t0 + width])
             raw.append(x_chunk)
-            if i == 2:
+            if i == 1:
                 nc.sync.dma_start(gather_list[:], offs)
                 nc.sync.dma_start(scatter_list[:], dst)
 
@@ -57,15 +58,15 @@ def tile_moe_two_lin_none_kernel(tc, xT, w_words, w_scales, gate, offs, dst, out
             nc.sync.dma_start(w_plane[32 * s : 32 * s + 4].bitcast(I32), scale_rows[s].bitcast(I32))
         w_codes = []
         gates = []
-        for e in range(E):
-            w_code = keep.tile([P, PASSES, N], U32, align_bytes=256, name=f"w_code{e}")
-            nc.sync.dma_start(w_code[:].bitcast(I32), w_words[e].rearrange("a p n r -> p a (n r)").bitcast(I32))
+        per_part = E // PARTS
+        for h in range(PARTS):
+            w_code = keep.tile([P, per_part * PASSES, N], U32, align_bytes=256, name=f"w_code{h}")
+            words = w_words[h * per_part : (h + 1) * per_part].rearrange("e a p n r -> p (e a) (n r)")
+            nc.sync.dma_start(w_code[:].bitcast(I32), words.bitcast(I32))
             w_codes.append(w_code)
-            if e % 3 == 2:
-                h = e // 3
-                gate_half = keep.tile([P, half], F32, align_bytes=256, name=f"gate_half{h}")
-                nc.sync.dma_start(gate_half[:], gate[:, h * half : (h + 1) * half])
-                gates.append(gate_half)
+            gate_part = keep.tile([P, part], F32, align_bytes=256, name=f"gate_part{h}")
+            nc.sync.dma_start(gate_part[:], gate[:, h * part : (h + 1) * part])
+            gates.append(gate_part)
 
         codes = []
         for a in range(PASSES):
@@ -94,11 +95,15 @@ def tile_moe_two_lin_none_kernel(tc, xT, w_words, w_scales, gate, offs, dst, out
 
         def quantize_chunk(i):
             a, t0, width, v = CHUNKS[i]
-            nc.vector.quantize_mx(
-                out=codes[a][:, t0 : t0 + width].bitcast(FP8X4),
-                scales=plane[4 * a : P, t0 : t0 + width],
-                in_=grouped[i][:].rearrange("p w j -> p (w j)"),
-            )
+            done = 0
+            while done < width:
+                step = min(512, width - done)
+                nc.vector.quantize_mx(
+                    out=codes[a][:, t0 + done : t0 + done + step].bitcast(FP8X4),
+                    scales=plane[4 * a : P, t0 + done : t0 + done + step],
+                    in_=grouped[i][:, done : done + step, :].rearrange("p w j -> p (w j)"),
+                )
+                done += step
             if t0 + width == T and a < PASSES - 1:
                 nc.vector.tensor_copy(slot_codes[a][:], codes[a][:].indirect(gather_list[:]))
 
@@ -109,29 +114,40 @@ def tile_moe_two_lin_none_kernel(tc, xT, w_words, w_scales, gate, offs, dst, out
         quantize_chunk(len(CHUNKS) - 1)
 
         last = PASSES - 1
-        for h in range(2):
-            cols = slice(h * half, (h + 1) * half)
-            entries = slice(h * half // 16, (h + 1) * half // 16)
-            nc.vector.tensor_copy(slot_codes[last][:, cols], codes[last][:].indirect(gather_list[:, entries]))
-            nc.vector.tensor_copy(slot_plane[:, cols], plane[:].indirect(gather_list[:, entries]))
-        for h in range(2):
-            acc = psum.tile([P, half], F32, name=f"acc{h}")
-            for local in range(3):
-                e = 3 * h + local
+        ys = []
+
+        def entries(h):
+            return slice(h * part // 16, (h + 1) * part // 16)
+
+        def multiply(h):
+            cols = slice(h * part, (h + 1) * part)
+            nc.vector.tensor_copy(slot_codes[last][:, cols], codes[last][:].indirect(gather_list[:, entries(h)]))
+            nc.vector.tensor_copy(slot_plane[:, cols], plane[:].indirect(gather_list[:, entries(h)]))
+            acc = psum.tile([P, part], F32, name=f"acc{h}")
+            for local in range(per_part):
+                e = per_part * h + local
                 slots = slice(e * C, (e + 1) * C)
                 for a in range(PASSES):
                     nc.tensor.matmul_mx(
                         out=acc[:, local * C : (local + 1) * C],
-                        lhsT=w_codes[e][:, a, :].bitcast(FP8X4),
+                        lhsT=w_codes[h][:, PASSES * local + a, :].bitcast(FP8X4),
                         lhsT_scale=w_plane[:, PASSES * e + a, :],
                         rhs=slot_codes[a][:, slots].bitcast(FP8X4),
                         rhs_scale=slot_plane[4 * a : P, slots],
                         start=(a == 0),
                         stop=(a == PASSES - 1),
                     )
-            y = keep.tile([P, half], F32, align_bytes=256, name=f"y{h}")
+            y = keep.tile([P, part], F32, align_bytes=256, name=f"y{h}")
             nc.scalar.activation(y[:], acc[:], COPY)
-            nc.vector.tensor_tensor(
-                result[:].indirect(scatter_list[:, h * half // 16 : (h + 1) * half // 16]), y[:], gates[h][:], MULT
-            )
+            ys.append(y)
+
+        def place(h):
+            nc.vector.tensor_tensor(result[:].indirect(scatter_list[:, entries(h)]), ys[h][:], gates[h][:], MULT)
+
+        multiply(0)
+        multiply(1)
+        place(0)
+        multiply(2)
+        place(1)
+        place(2)
         nc.sync.dma_start(out, result[:])

@@ -19,9 +19,17 @@ MULT = mybir.AluOpType.mult
 FLOPS = 2 * K * S * N
 
 CHUNKS = (
-    (0, 0, 768, 192), (0, 768, 768, 192),
-    (1, 0, 768, 192), (1, 768, 768, 192),
-    (2, 0, 768, 192), (2, 768, 512, 256), (2, 1280, 256, 160),
+    (0, 0, 256, 64),
+    (0, 256, 256, 64),
+    (0, 512, 512, 128),
+    (0, 1024, 512, 128),
+    (1, 0, 512, 128),
+    (1, 512, 512, 128),
+    (1, 1024, 512, 128),
+    (2, 0, 512, 128),
+    (2, 512, 512, 128),
+    (2, 1024, 256, 128),
+    (2, 1280, 256, 160),
 )
 PARTS = 3
 

@@ -59,7 +59,6 @@ def tile_moe_two_lin_none_kernel(tc, xT, w_words, w_scales, gate, offs, dst, out
             raw.append(x_chunk)
             if i == 1:
                 nc.sync.dma_start(gather_list[:], offs)
-                nc.sync.dma_start(scatter_list[:], dst)
 
         scale_rows = w_scales.rearrange("e a (s r) n -> s r (e a) n", r=4)
         for s in range(4):
@@ -75,6 +74,8 @@ def tile_moe_two_lin_none_kernel(tc, xT, w_words, w_scales, gate, offs, dst, out
             gate_part = keep.tile([P, part], F32, align_bytes=256, name=f"gate_part{h}")
             nc.sync.dma_start(gate_part[:], gate[:, h * part : (h + 1) * part])
             gates.append(gate_part)
+            if h == 0:
+                nc.sync.dma_start(scatter_list[:], dst)
 
         codes = []
         for a in range(PASSES):
@@ -97,7 +98,8 @@ def tile_moe_two_lin_none_kernel(tc, xT, w_words, w_scales, gate, offs, dst, out
         def round_chunk(i):
             a, t0, width, v = CHUNKS[i]
             group = keep.tile([P, width, PACK], BF16, align_bytes=256, name=f"group{i}")
-            nc.scalar.activation(interleaved(group[:, v:width, :]), by_four(raw[i][:, :, v:width]), COPY)
+            if v < width:
+                nc.scalar.activation(interleaved(group[:, v:width, :]), by_four(raw[i][:, :, v:width]), COPY)
             nc.vector.tensor_copy(interleaved(group[:, 0:v, :]), by_four(raw[i][:, :, 0:v]))
             grouped.append(group)
 
@@ -105,7 +107,7 @@ def tile_moe_two_lin_none_kernel(tc, xT, w_words, w_scales, gate, offs, dst, out
             a, t0, width, v = CHUNKS[i]
             done = 0
             while done < width:
-                step = min(512, width - done)
+                step = max(w for w in (128, 256, 512) if w <= width - done)
                 nc.vector.quantize_mx(
                     out=codes[a][:, t0 + done : t0 + done + step].bitcast(FP8X4),
                     scales=plane[4 * a : P, t0 + done : t0 + done + step],
@@ -124,13 +126,15 @@ def tile_moe_two_lin_none_kernel(tc, xT, w_words, w_scales, gate, offs, dst, out
         last = PASSES - 1
         ys = []
 
-        def entries(h):
-            return slice(h * part // 16, (h + 1) * part // 16)
+        def entries(first, end):
+            return slice(first // 16, end // 16)
+
+        def gather_last(first, end):
+            cols = slice(first, end)
+            nc.vector.tensor_copy(slot_codes[last][:, cols], codes[last][:].indirect(gather_list[:, entries(first, end)]))
+            nc.vector.tensor_copy(slot_plane[:, cols], plane[:].indirect(gather_list[:, entries(first, end)]))
 
         def multiply(h):
-            cols = slice(h * part, (h + 1) * part)
-            nc.vector.tensor_copy(slot_codes[last][:, cols], codes[last][:].indirect(gather_list[:, entries(h)]))
-            nc.vector.tensor_copy(slot_plane[:, cols], plane[:].indirect(gather_list[:, entries(h)]))
             acc = psum.tile([P, part], F32, name=f"acc{h}")
             for local in range(per_part):
                 e = per_part * h + local
@@ -149,13 +153,13 @@ def tile_moe_two_lin_none_kernel(tc, xT, w_words, w_scales, gate, offs, dst, out
             nc.scalar.activation(y[:], acc[:], COPY)
             ys.append(y)
 
-        def place(h):
-            nc.vector.tensor_tensor(result[:].indirect(scatter_list[:, entries(h)]), ys[h][:], gates[h][:], MULT)
-
+        gather_last(0, part)
         multiply(0)
-        multiply(1)
-        place(0)
-        multiply(2)
-        place(1)
-        place(2)
+        gather_last(part, S)
+        for h in range(1, PARTS):
+            multiply(h)
+        for h in range(PARTS):
+            nc.vector.tensor_tensor(
+                result[:].indirect(scatter_list[:, entries(h * part, (h + 1) * part)]), ys[h][:], gates[h][:], MULT
+            )
         nc.sync.dma_start(out, result[:])

import concourse.mybir as mybir

E, C, K, T, N = 6, 128, 1536, 1536, 128
S = E * C
P = 128
PACK = 4
PASSES = 3

F32 = mybir.dt.float32
BF16 = mybir.dt.bfloat16
U32 = mybir.dt.uint32
I32 = mybir.dt.int32
U16 = mybir.dt.uint16
U8 = mybir.dt.uint8
FP8X4 = mybir.dt.float8_e4m3fn_x4
COPY = mybir.ActivationFunctionType.Copy
MULT = mybir.AluOpType.mult

FLOPS = 2 * K * S * N

CHUNKS = (
    (0, 0, 256, 64),
    (0, 256, 256, 64),
    (0, 512, 512, 128),
    (0, 1024, 512, 128),
    (1, 0, 512, 128),
    (1, 512, 512, 128),
    (1, 1024, 512, 128),
    (2, 0, 512, 128),
    (2, 512, 512, 128),
    (2, 1024, 256, 128),
    (2, 1280, 256, 160),
)
PARTS = 3


def tile_moe_two_lin_none_kernel(tc, xT, w_words, w_scales, gate, offs, dst, out):
    nc = tc.nc
    part = S // PARTS
    with (
        tc.tile_pool(name="keep", bufs=1) as keep,
        tc.psum_pool(name="psum", bufs=1) as psum,
    ):
        gather_list = keep.tile([P, S // 16], U16, name="gather_list")
        scatter_list = keep.tile([P, S // 16], U16, name="scatter_list")

        w_plane = keep.tile([P, E * PASSES, N], U8, align_bytes=256, name="w_plane")
        plane = keep.tile([P, T], U8, align_bytes=256, name="plane")
        result = keep.tile([P, T], F32, align_bytes=256, name="result")
        nc.vector.memset(w_plane[:].bitcast(I32), 0)
        nc.gpsimd.memset(plane[:], 0)
        nc.gpsimd.memset(result[:], 0.0)

        x_view = xT.rearrange("(a p j) t -> a p j t", a=PASSES, j=PACK)
        raw = []
        for i, (a, t0, width, vector_width) in enumerate(CHUNKS):
            x_chunk = keep.tile([P, PACK, width], F32, align_bytes=256, name=f"x_chunk{i}")
            nc.sync.dma_start(x_chunk[:], x_view[a, :, :, t0 : t0 + width])
            raw.append(x_chunk)
            if i == 1:
                nc.sync.dma_start(gather_list[:], offs)

        scale_rows = w_scales.rearrange("e a (s r) n -> s r (e a) n", r=4)
        for s in range(4):
            nc.sync.dma_start(w_plane[32 * s : 32 * s + 4].bitcast(I32), scale_rows[s].bitcast(I32))
        w_codes = []
        gates = []
        per_part = E // PARTS
        for h in range(PARTS):
            w_code = keep.tile([P, per_part * PASSES, N], U32, align_bytes=256, name=f"w_code{h}")
            words = w_words[h * per_part : (h + 1) * per_part].rearrange("e a p n r -> p (e a) (n r)")
            nc.sync.dma_start(w_code[:].bitcast(I32), words.bitcast(I32))
            w_codes.append(w_code)
            gate_part = keep.tile([P, part], F32, align_bytes=256, name=f"gate_part{h}")
            nc.sync.dma_start(gate_part[:], gate[:, h * part : (h + 1) * part])
            gates.append(gate_part)
            if h == 0:
                nc.sync.dma_start(scatter_list[:], dst)

        codes = []
        for a in range(PASSES):
            pass_codes = keep.tile([P, T], U32, align_bytes=256, name=f"pass_codes{a}")
            codes.append(pass_codes)
        slot_codes = []
        for a in range(PASSES):
            slot_code = keep.tile([P, S], U32, align_bytes=256, name=f"slot_code{a}")
            slot_codes.append(slot_code)
        slot_plane = keep.tile([P, S], U8, align_bytes=256, name="slot_plane")

        def interleaved(ap):
            return ap.rearrange("p (c i) j -> p c j i", i=4)

        def by_four(ap):
            return ap.rearrange("p j (c i) -> p c j i", i=4)

        grouped = []

        def round_chunk(i):
            a, t0, width, v = CHUNKS[i]
            group = keep.tile([P, width, PACK], BF16, align_bytes=256, name=f"group{i}")
            if v < width:
                nc.scalar.activation(interleaved(group[:, v:width, :]), by_four(raw[i][:, :, v:width]), COPY)
            nc.vector.tensor_copy(interleaved(group[:, 0:v, :]), by_four(raw[i][:, :, 0:v]))
            grouped.append(group)

        def quantize_chunk(i):
            a, t0, width, v = CHUNKS[i]
            done = 0
            while done < width:
                step = max(w for w in (128, 256, 512) if w <= width - done)
                nc.vector.quantize_mx(
                    out=codes[a][:, t0 + done : t0 + done + step].bitcast(FP8X4),
                    scales=plane[4 * a : P, t0 + done : t0 + done + step],
                    in_=grouped[i][:, done : done + step, :].rearrange("p w j -> p (w j)"),
                )
                done += step
            if t0 + width == T and a < PASSES - 1:
                nc.vector.tensor_copy(slot_codes[a][:], codes[a][:].indirect(gather_list[:]))

        round_chunk(0)
        for i in range(1, len(CHUNKS)):
            round_chunk(i)
            quantize_chunk(i - 1)
        quantize_chunk(len(CHUNKS) - 1)

        last = PASSES - 1
        ys = []

        def entries(first, end):
            return slice(first // 16, end // 16)

        def gather_last(first, end):
            cols = slice(first, end)
            nc.vector.tensor_copy(slot_codes[last][:, cols], codes[last][:].indirect(gather_list[:, entries(first, end)]))
            nc.vector.tensor_copy(slot_plane[:, cols], plane[:].indirect(gather_list[:, entries(first, end)]))

        def multiply(h):
            acc = psum.tile([P, part], F32, name=f"acc{h}")
            for local in range(per_part):
                e = per_part * h + local
                slots = slice(e * C, (e + 1) * C)
                for a in range(PASSES):
                    nc.tensor.matmul_mx(
                        out=acc[:, local * C : (local + 1) * C],
                        lhsT=w_codes[h][:, PASSES * local + a, :].bitcast(FP8X4),
                        lhsT_scale=w_plane[:, PASSES * e + a, :],
                        rhs=slot_codes[a][:, slots].bitcast(FP8X4),
                        rhs_scale=slot_plane[4 * a : P, slots],
                        start=(a == 0),
                        stop=(a == PASSES - 1),
                    )
            y = keep.tile([P, part], F32, align_bytes=256, name=f"y{h}")
            nc.scalar.activation(y[:], acc[:], COPY)
            ys.append(y)

        gather_last(0, part)
        multiply(0)
        gather_last(part, S)
        for h in range(1, PARTS):
            multiply(h)
        for h in range(PARTS):
            nc.vector.tensor_tensor(
                result[:].indirect(scatter_list[:, entries(h * part, (h + 1) * part)]), ys[h][:], gates[h][:], MULT
            )
        nc.sync.dma_start(out, result[:])
